import numpy as np, ml_dtypes
CORES = [24,25,26,27,28,29,30,31]
N = 8
import mx_ref
BF = ml_dtypes.bfloat16
def gentries(a):
    return np.ascontiguousarray(a.reshape(8, 16, -1).transpose(0, 2, 1)).reshape(8, -1)
def gtable(e):
    e = np.asarray(e); return np.ascontiguousarray(e.reshape(8, -1, 16).transpose(0, 2, 1)).reshape(128, -1).astype(np.int32)
def gcols(t, e):
    v = np.concatenate([t.reshape(8, 16, -1, 4), np.zeros((8, 16, 1, 4), BF)], axis=2)
    return np.ascontiguousarray(np.stack([v[g][:, e[g]] for g in range(8)])).reshape(128, -1)
def tile(rs):
    return np.stack(rs, axis=2).reshape(128, -1).astype(BF)
def cut(t, i, w=512):
    return t[:, w * i:w * i + w]
def pick(q, e):
    c = np.concatenate([q[0].reshape(128, -1, 4), np.zeros((128, 1, 4), np.uint8)], axis=1); s = np.concatenate([q[1], np.ones((16, 1), np.uint8)], axis=1)
    return (np.ascontiguousarray(c[:, e].reshape(128, -1)), np.ascontiguousarray(s[:, e]))
def join(*qs):
    return (np.concatenate([q[0] for q in qs], axis=1), np.concatenate([q[1] for q in qs], axis=1))
def put(q, e, v):
    c, s = q[0].reshape(128, -1, 4).copy(), q[1].copy(); c[:, e] = v[0].reshape(128, -1, 4); s[:, e] = v[1]
    return (c.reshape(128, -1), s)
def pk(c, s):
    return (np.ascontiguousarray(c), mx_ref.live(s))
def emit(q):
    return q[0], q[1]
def packed(v, rng):
    q = [mx_ref.quantize(np.ascontiguousarray(v[r])) for r in range(N)]
    return np.stack([a for a, b in q]), np.stack([mx_ref.plane(b, rng) for a, b in q])
def values_of_codes():
    e, c = np.zeros((128, 128, 4), np.float32), np.zeros((128, 2, 4), np.uint8)
    e[np.arange(128), np.arange(128), 0] = 1
    c[:127, :, 0] = np.arange(256).reshape(2, 128).T[:127]
    return mx_ref.matmul(mx_ref.quantize(e.reshape(128, 512).astype(BF)), (c.reshape(128, 8), np.full((16, 2), 127, np.uint8))).T.reshape(-1).astype(np.float64)
CODE_VALUE, SCALE_VALUE = values_of_codes(), 2.0 ** (np.arange(256) - 127.0)
def decode(q):
    return (CODE_VALUE[q[0]].reshape(16, 8, -1, 4) * SCALE_VALUE[q[1]][:, None, :, None] + 0.0).reshape(128, -1).astype(np.float32)
def f(rng, *shape):
    return mx_ref.flush((rng.standard_normal(shape, dtype=np.float32) * np.exp2(rng.integers(-2, 3, shape[:-1] + (1,)))).astype(BF))
def wide(rng, *shape, cols=0):
    v = rng.standard_normal(shape, dtype=np.float32) * np.exp2(rng.integers(-12, 13, shape)).astype(np.float32)
    if cols: v *= np.repeat(np.exp2(rng.integers(-cols, cols + 1, shape[:-2] + (1, shape[-1] // 4))) * (rng.random(shape[:-2] + (1, shape[-1] // 4)) > 0.0625), 4, axis=-1).astype(np.float32)
    return mx_ref.flush(v.astype(BF))
C, A, R = 256, 64, 3
def order(p):
    return np.argsort(-(p + np.float32(0.0)), axis=1, kind="stable")
def means(t, a, x, b):
    return ((gcols(t, a).astype(np.float32) + gcols(x, b).astype(np.float32)) * np.float32(0.5)).astype(BF)
def along(o, e):
    return np.take_along_axis(o, e, axis=1)
def big(v):
    v = v.astype(np.float32)
    v[np.abs(v) < np.float32(2.0 ** -16)] = 0
    return v.astype(BF)
def families(rng):
    return np.stack([big(f(rng, N, 128, 4 * A)) for i in range(2)])
def lists_of(rng):
    return rng.integers(0, A, (2, N, 8, C)), rng.integers(0, C, (2, N, 8, C))
def others(rng):
    k = rng.integers(0, A - 8, (2, N, 8, C))
    return k + k // 7 + 1
def layers(rng, still=()):
    w = big(f(rng, N, 128, 2048)).reshape(N, 8, 16, 4, 8, 16, 4)
    for i in still:
        w[:, :, i] = 0
        w[:, :, :, :, :, i] = 0
    return w
def made(rng, x, s, a, b, w):
    c, p = packed(np.ascontiguousarray(w).reshape(N, 128, 2048), rng)
    x, s = np.ascontiguousarray(x).reshape(N, 128, 4 * C), np.ascontiguousarray(s).reshape(2, N, 128, 4 * A)
    t = [np.stack([gtable(e) for e in k]) for k in (a[0], b[0], a[1], b[1])]
    return {"x": x, "l0": s[0], "r0": s[1], "la": t[0], "lx": t[1], "ra": t[2], "rx": t[3], "wc": c, "ws": p, "v": np.array(f(rng, N, 128, 512))}
def signs(rng):
    return np.stack([rng.permutation(8) % 2 * 2.0 - 1.0 for r in range(N)])
def setup_inputs(rng):
    a, b = lists_of(rng)
    return made(rng, big(f(rng, N, 128, 4 * C)), families(rng), a, b, layers(rng))
def setup_inputs_ties(rng):
    x = big(f(rng, N, 128, 4 * C)).reshape(N, 8, 16, C, 4)
    s = families(rng).reshape(2, N, 8, 16, A, 4)
    keep = s[:, :, :, :8, 0].copy()
    e = rng.permutation(N)
    for r in range(N):
        for t in (x[r], s[0, r], s[1, r]):
            n = t.shape[2]
            k = np.zeros(n, int) if r == e[0] else rng.permutation(n) % 3
            m = t[:, :8, :3].copy()
            m[:, :, 2] = 0
            t[:, :8] = m[:, :, k]
    x[e[1]] = 0
    s[:, :, :, :, ::8] = 0
    for h in range(8): s[:, :, h, :8, 8 * h] = keep[:, :, h]
    a, b = lists_of(rng)
    return made(rng, x, s, a, b, layers(rng, range(8)))
def setup_inputs_near(rng):
    x, s = np.zeros((N, 8, 16, C, 4)), np.zeros((2, N, 8, 16, A, 4))
    a, b = others(rng), np.zeros((2, N, 8, C), int)
    o, c = rng.permutation(N) % 4, signs(rng)
    j = np.arange(C)
    g = ((((j + 1) // 2)[:, None] >> np.arange(8)) & 1) * np.exp2(np.arange(8) - 22.0)
    for r in range(N):
        size = 1.0 if o[r] < 2 else 2.0 ** -4
        if o[r] < 2:
            x[r, :, 0, :, 0] = 2 * c[r][:, None]
            for h in rng.permutation(8)[:4]: x[r, h, 0, C - 1 if c[r, h] > 0 else 0, 0] *= 2.0 ** 29
        if o[r] == 3: x[r, :, 0, :, 0] = (8 + j % 2) * 2.0 ** -29
        x[r, :, 8] = g[:, :4] * size
        x[r, :, 9] = g[:, 4:] * size
        x[r, :, 10:] = rng.integers(4, 8, (8, 6, C, 4)) * 2.0 ** -19 * size
        s[:, r, :, 10:] = rng.integers(4, 8, (2, 8, 6, A, 4)) * 2.0 ** -19 * size
        s[:, r, :, :, ::8] = 0
        k = 1.0 if o[r] == 0 else 2.0 ** -30
        for h in range(8):
            s[:, r, h, 0, 8 * h, 0] = k
            s[:, r, h, 8:10, 8 * h] = k
        m = rng.integers(0, C, (2, 8, 1))
        b[:, r] = (j + m) % (C // 2) * 2 + j // (C // 2) if o[r] == 3 else (j + m) % C
    return made(rng, x.astype(np.float32).astype(BF), s.astype(np.float32).astype(BF), a, b, layers(rng, range(10)))
def setup_inputs_huge(rng):
    one = rng.permutation(N) < N // 2
    n = N - N // 2
    def full(*shape):
        k = 1 - 0.04 * rng.random(shape + (4,))
        k[..., ::8, :, 0] = 1
        return k
    j = np.arange(C)
    c = np.where(one[:, None] | (j >= C // 2), -1.0, 1.0)
    x = 0.6 + 0.2 * rng.random((N, 128, C, 4))
    x[~one] = full(n, 128, C)
    x *= 2.0 ** 30 * c[:, None, :, None]
    s = -(0.6 + 0.2 * rng.random((2, N, 128, A, 4)))
    s[:, ~one] = full(2, n, 128, A) * np.where(np.arange(A) < A // 2, 1.0, -1.0)[:, None]
    q = 1 - 0.25 * rng.random((2, N, 128, 8, 4))
    q[:, ~one] = full(2, n, 128, 8)
    s[:, :, :, ::8] = q * np.stack([signs(rng), signs(rng)])[:, :, None, :, None]
    s *= 2.0 ** 30
    k = (np.argsort(rng.random((2, N, 1, C)), axis=3) >= A // 2).astype(int)
    b = k * (C // 2) + rng.integers(0, C // 2, (2, N, 8, C))
    m = rng.integers(0, A // 2 - 4, (2, N, 8, C))
    a = np.where(one[:, None, None], others(rng), k * (A // 2) + m + m // 7 + 1)
    w = np.zeros((N, 128, 4, 128, 4), np.float32)
    i = np.arange(128)
    for h in range(4): w[:, i, h, i, h] = -16
    return made(rng, x.astype(np.float32).astype(BF), s.astype(np.float32).astype(BF), a, b, w.astype(BF))
def setup_inputs_lists(rng):
    def shapes(n):
        i = np.arange(C)
        k = [np.zeros(C, int), np.full(C, n - 1), i % n, n - 1 - i % n, i * n // C, rng.permutation(C) % n, rng.permutation(n)[i % 2], rng.integers(0, n, C)]
        return np.stack(k)[rng.permutation(8)]
    a, b = [np.stack([np.stack([shapes(n) for r in range(N)]) for i in range(2)]) for n in (A, C)]
    e = int(rng.integers(N))
    a[:, e] = rng.integers(0, A, (2, 8, 1))
    b[:, e] = rng.integers(0, C, (2, 8, 1))
    return made(rng, big(f(rng, N, 128, 4 * C)), families(rng), a, b, layers(rng))
def setup_inputs_spread(rng):
    a, b = lists_of(rng)
    return made(rng, big(wide(rng, N, 128, 4 * C, cols=6)), np.stack([big(wide(rng, N, 128, 4 * A)) for i in range(2)]), a, b, layers(rng))
def check_inputs(d):
    b = []
    for k in ("x", "l0", "r0", "v"):
        a = np.abs(d[k].astype(np.float32))
        if not (np.isfinite(a).all() and ((a == 0) | (a >= 2.0 ** -30) & (a <= 2.0 ** 30)).all()): b.append("a value of " + k)
    for k, n in (("la", A), ("lx", C), ("ra", A), ("rx", C)):
        if not ((d[k] >= 0) & (d[k] < n)).all(): b.append("an entry of " + k)
    if ((d["wc"] & 0x7F) == 0x7F).any(): b.append("a code of wc that is no number")
    z = np.zeros((128, 4, 4), np.float32)
    z[:, 1] = 2.0 ** -30
    z[:, 2] = 2.0 ** 30
    c, s = emit(mx_ref.quantize(z.reshape(128, 16).astype(BF)))
    for r in range(N):
        p = mx_ref.live(d["ws"][r])
        if not ((p == s[0, 0]) | (p >= s[0, 1]) & (p <= s[0, 2])).all(): b.append("a scale of ws")
    return b
def reference(x, l0, r0, la, lx, ra, rx, wc, ws, v):
    lay = [pk(wc[r], ws[r]) for r in range(N)]
    left, right = [l0[r] for r in range(N)], [r0[r] for r in range(N)]
    ol = [np.tile(A * r + np.arange(A), (8, 1)) for r in range(N)]
    og = [k.copy() for k in ol]
    for t in range(R):
        sent, pl, pg = [], [], []
        for r in range(N):
            a, c = gentries(la[r]), gentries(ra[r])
            z, w = means(left[r], a, x[r], gentries(lx[r])), means(right[r], c, x[r], gentries(rx[r]))
            q = mx_ref.quantize(np.concatenate([right[r], left[r]], axis=1))
            e = order(mx_ref.matmul(q, mx_ref.quantize(z))[:A:8])[:, :A]
            h = order(mx_ref.matmul(q, mx_ref.quantize(w))[A::8])[:, :A]
            sent.append(mx_ref.quantize(np.concatenate([gcols(z, e), gcols(w, h)], axis=1)))
            pl.append(along(along(ol[r], a), e))
            pg.append(along(along(og[r], c), h))
        came = decode(join(*sent)).astype(BF)
        for r in range(N):
            i, j = (r - 1) % N, (r + 1) % N
            got = np.concatenate([cut(came, 2 * i, 4 * A), cut(came, 2 * j + 1, 4 * A)], axis=1)
            q = mx_ref.quantize(got)
            new = tile([np.maximum(mx_ref.matmul(pick(lay[r], np.arange(128 * b, 128 * b + 128)), q), np.float32(0.0)) * np.float32(0.03125) + got[:, b::4].astype(np.float32) for b in range(4)])
            left[r], right[r] = new[:, :4 * A], new[:, 4 * A:]
            ol[r], og[r] = pl[i], pg[j]
    y, ot = np.zeros((N, 128, 2 * A), np.float32), np.zeros((N, 8, 2 * A), np.float32)
    oc, osc = np.zeros((N, 128, 8 * A), np.uint8), np.zeros((N, 16, 2 * A), np.uint8)
    for r in range(N):
        q = mx_ref.quantize(np.concatenate([left[r], right[r]], axis=1))
        y[r] = mx_ref.matmul(mx_ref.quantize(v[r]), q)
        ot[r] = np.concatenate([ol[r], og[r]], axis=1)
        oc[r], osc[r] = emit(q)
    return {"y": y, "ot": ot, "oc": oc, "osc": osc}

@@ -1,0 +1,397 @@
+from concourse.bass import DstId, RemoteDMATransfer
+from concourse.mybir import dt, AluOpType, AxisListType, ActivationFunctionType
+
+ROUNDS = 3
+CFG = {"ns": 4, "cuts": [0, 4, 8], "unpack": 3, "early": 2}
+_SIGNED = [(3, 0), (4, 0), (7, 0), (6, 0), (5, 0), (2, 0), (1, 4)]
+PLAN = ([("decide", 0, 0, 4), ("decide", 1, 0, 4)] + [("signs", q, lo, 8) for q, lo in _SIGNED] +
+        [("direct", 0, 4, 8), ("count", 0, 0, 0)] +
+        [(step, q, lo, 8) for q, lo in _SIGNED for step in ("decide", "count")])
+X4, U8, BF, F32, I32, U16 = "float8_e4m3fn_x4", "uint8", "bfloat16", "float32", "int32", "uint16"
+
+
+def _sb(n, d):
+    return ("sbuf", [128, n], d)
+
+
+SCRATCH = {
+    "xs": _sb(1024, BF), "b0": _sb(512, BF), "vs": _sb(512, BF), "lab": _sb(32, I32), "lxb": _sb(32, I32),
+    "qw": _sb(512, X4), "sw": _sb(512, U8), "qv": _sb(128, X4), "sv": _sb(128, U8),
+    "pint": _sb(1, I32), "pb": _sb(8, I32), "pf": _sb(8, F32), "pc": _sb(16, F32),
+    "jrow": _sb(128, F32), "pat": _sb(64, F32), "taui": _sb(128, F32), "tau": _sb(128, BF),
+    "ci": _sb(512, BF), "ct": _sb(512, BF), "qc": _sb(128, X4), "sc": _sb(128, U8),
+    "et": _sb(2048, BF), "qe": _sb(512, X4), "se": _sb(512, U8),
+    "cb": _sb(8, F32), "base": _sb(128, F32),
+    "a16": _sb(32, F32), "a8": _sb(32, I32), "a127": _sb(32, F32), "asum": _sb(32, F32),
+    "offa": _sb(32, U16), "offx": _sb(128, U16), "offb": _sb(32, U16), "offs": _sb(16, U16), "offp": _sb(2, U16),
+    "offn": _sb(8, U16), "offm": _sb(32, U16), "offf": _sb(8, U16),
+    "xh": _sb(2048, BF), "bh": _sb(576, BF), "zy": _sb(2048, BF), "st": _sb(1024, BF),
+    "qs": _sb(256, X4), "ss": _sb(256, U8),
+    "rows": _sb(256, F32), "piv": _sb(32, F32), "sig": _sb(8192, BF), "qg": _sb(2048, X4), "sg": _sb(2048, U8),
+    "rk": _sb(256, BF), "dif": _sb(2048, BF), "run": _sb(2048, BF), "ones": _sb(1024, BF), "lsum": _sb(8, F32),
+    "dp": _sb(2048, BF), "ft": _sb(512, BF), "fh": _sb(512, BF), "qf": _sb(128, X4), "sf": _sb(128, U8),
+    "rl": _sb(512, F32), "bt": _sb(512, BF), "qb": _sb(128, X4), "sb": _sb(128, U8), "yb": _sb(128, F32),
+    "org": _sb(128, BF), "ozy": _sb(512, BF), "oin": _sb(512, BF), "otb": _sb(128, F32),
+    "oout": ("dram", [2 * ROUNDS, 128, 16], BF), "oland": ("dram", [2 * ROUNDS, 128, 16], BF),
+    "pss": ("psum", [128, 1024], F32), "psr": ("psum", [128, 512], F32), "psd": ("psum", [128, 2048], F32),
+}
+SEMAPHORES = ["cv", "cs", "cp", "cg", "sent", "ldx", "ldlx", "ldla", "ldb", "ldw", "ldv", "sty", "sto", "stc"]
+for _t in range(ROUNDS):
+    SCRATCH["qzy%d" % _t] = _sb(512, X4)
+    SCRATCH["szy%d" % _t] = _sb(512, U8)
+    SCRATCH["qin%d" % _t] = _sb(512, X4)
+    SCRATCH["sin%d" % _t] = _sb(512, U8)
+    SCRATCH["lst%d" % _t] = _sb(16, BF)
+    SCRATCH["lin%d" % _t] = _sb(16, BF)
+    SEMAPHORES += ["ac%d" % _t, "ao%d" % _t, "al%d" % _t, "oa%d" % _t, "ob%d" % _t]
+
+
+def rank_program(g, core, T, topo):
+    rank = T.rank_of(core)
+    if rank is None:
+        return
+    n_ranks = len(T.cores)
+    nxt, prv = T.cores[(rank + 1) % n_ranks], T.cores[(rank - 1) % n_ranks]
+    A, ACT = AluOpType, ActivationFunctionType
+    V, S, P, Y = g.vector, g.scalar, g.tensor, g.sync
+    queue = {"v": V, "s": S, "p": P, "g": g, "y": Y}
+    total, waited, wrote, read = {}, {}, {}, {}
+
+    def settle(q, r, w):
+        need = {}
+        toks = [wrote[k] for k in list(r) + list(w) if k in wrote]
+        for k in w:
+            toks += read.get(k, [])
+        for sem, val in toks:
+            if not (q == "p" and sem == "cp"):
+                need[sem] = max(need.get(sem, 0), val)
+        for sem, val in need.items():
+            if waited.get((q, sem), 0) < val:
+                queue[q].wait_ge(T.sem[sem], val)
+                waited[(q, sem)] = val
+
+    def note(tok, r, w):
+        for k in r:
+            read.setdefault(k, []).append(tok)
+        for k in w:
+            wrote[k] = tok
+            read[k] = []
+
+    def op(q, r, w, fn, *args, **kw):
+        settle(q, r, w)
+        sem = "c" + q
+        total[sem] = total.get(sem, 0) + 1
+        fn(*args, **kw).then_inc(T.sem[sem], 1)
+        note((sem, total[sem]), r, w)
+
+    def dmas(q, sem, r, w, pairs):
+        settle(q, r, w)
+        for out, in_ in pairs:
+            queue[q].dma_start(out, in_).then_inc(T.sem[sem], 16)
+        total[sem] = total.get(sem, 0) + 16 * len(pairs)
+        note((sem, total[sem]), r, w)
+
+    def half_mask(dst, upper):
+        e = topo.engines(core, dst)
+        h = len(e) // 2
+        return sum(1 << k for k in (e[h:] if upper else e[:h])), h
+
+    def send(sem, r, arrives, up, down):
+        settle("g", r, [])
+        ts, n = [], 0
+        for dst, (src, land), upper in ((nxt, up, False), (prv, down, True)):
+            rid, pid, _ = topo.addr(dst)
+            m, h = half_mask(dst, upper)
+            n += h
+            ts.append(RemoteDMATransfer(dst_ids=[DstId(rid=rid, pnc=pid)], dma_engine_mask=m, remote_sem=T.sem[sem],
+                                        src=src, dst=land))
+        g.remote_dma_fused(ts, local_sem=T.sem.sent)
+        total["sent"] = total.get("sent", 0) + n
+        total[sem] = total.get(sem, 0) + n
+        wrote[arrives] = (sem, total[sem])
+
+    def u8(view):
+        return view.bitcast(dt.uint8)
+
+    def halves(out, left, right):
+        return [(out[:, 16 * h + 8 * f:16 * h + 8 * f + 8], (left, right)[f][:, 8 * h:8 * h + 8])
+                for h in range(2) for f in range(2)]
+
+    dmas("s", "ldx", [], ["xs"], [(T.xs[:], T.x[:])])
+    dmas("y", "ldlx", [], ["lxb"], halves(T.lxb, T.lx, T.rx))
+    dmas("s", "ldb", [], ["b0"], [(T.b0[:, 0:256], T.l0[:]), (T.b0[:, 256:512], T.r0[:])])
+    dmas("y", "ldla", [], ["lab"], halves(T.lab, T.la, T.ra))
+    dmas("y", "ldw", [], ["qw"], [(u8(T.qw[:]), T.wc[:]), (T.sw[:], T.ws[:])])
+    dmas("y", "ldv", [], ["vs"], [(T.vs[:], T.v[:])])
+
+    small = dict(allow_small_or_imprecise_dtypes=True)
+    op("g", [], ["pint"], g.iota, T.pint[:], [[0, 1]], 0, 1)
+    op("g", [], ["pat"], g.iota, T.pat[:, 0:32], [[1, 4], [4, 8]], 0, 0, **small)
+    op("g", [], ["taui"], g.iota, T.taui[:], [[1, 32], [-8, 4]], 0, 0, **small)
+    op("g", [], ["jrow"], g.iota, T.jrow[:], [[1, 128]], 0, 0, **small)
+    op("g", [], ["org"], g.iota, T.org[:], [[1, 8], [0, 2], [8, 8]], 0, 0, **small)
+    op("g", [], ["ci"], g.iota, T.ci[:], [[1, 8], [8, 2], [0, 32]], 0, 0, **small)
+    op("g", [], ["pat2"], g.iota, T.pat[:, 32:64], [[1, 4], [8, 8]], 0, 0, **small)
+    op("g", [], ["oin"], g.iota, T.oin[:], [[0, 512]], 0, 0, **small)
+    op("g", [], ["et"], g.iota, T.et[:], [[0, 2048]], 0, 0, **small)
+
+    def pf(c):
+        return T.pf[:, c:c + 1]
+
+    def pc(c):
+        return T.pc[:, c:c + 1]
+
+    planes = ["bh%d" % b for b in range(4)]
+    op("v", [], planes, V.memset, T.bh[:], 0.0)
+    for c, (sh, m) in enumerate(((0, 15), (4, 7), (0, 7), (3, 1), (0, 127))):
+        op("v", ["pint"], ["pb%d" % c], V.tensor_scalar, T.pb[:, c:c + 1], T.pint[:], sh, m,
+           A.logical_shift_right, A.bitwise_and)
+    op("v", ["pb%d" % c for c in range(5)], ["pf"], V.tensor_copy, T.pf[:, 0:5], T.pb[:, 0:5])
+    for c, a, m, b in ((0, 0, 32.0, 0.0), (2, 0, 8.0, pf(1)), (3, 2, 16.0, pf(3)), (4, 2, 8192.0, 0.0),
+                       (6, 3, 256.0, 0.0), (8, 3, 128.0, 0.0), (9, 3, -128.0, 128.0), (10, 0, 1.0, 8.0),
+                       (11, 0, 1.0, -8.0), (12, 3, 1.0, -1.0), (13, 3, -256.0, 256.0), (14, 3, -1.0, 0.0)):
+        op("v", ["pf"], ["pc%d" % c], V.tensor_scalar, pc(c), pf(a), m, b, A.mult, A.add)
+    op("v", ["pat", "pc0"], ["offb"], V.tensor_scalar, T.offb[:], T.pat[:, 0:32], pc(0), None, A.add)
+    for c in range(2):
+        op("v", planes + ["pc%d" % (8 + c), "pc%d" % (10 + c)], ["offs%d" % c], V.tensor_scalar,
+           T.offs[:, 8 * c:8 * c + 8], T.bh[:, 0:8], pc(10 + c), pc(8 + c), A.add, A.max)
+    op("v", ["pc2"], ["offp"], V.tensor_copy, T.offp[:, 0:1], pc(2))
+    op("v", ["taui", "pf"], ["taui"], V.tensor_scalar, T.taui[:], T.taui[:], pf(1), 0.0, A.subtract, A.is_gt)
+    for b in range(4):
+        op("v", ["lxb"], ["offx%d" % b], V.tensor_scalar, T.offx[:, 32 * b:32 * b + 32], T.lxb[:], 4.0, float(b),
+           A.mult, A.add)
+    op("v", ["lab"], ["a8"], V.tensor_scalar, T.a8[:], T.lab[:], 3, None, A.logical_shift_right)
+    for c in range(4):
+        op("v", ["lab"], ["a16_%d" % c], V.tensor_scalar, T.a16[:, 8 * c:8 * c + 8], T.lab[:, 8 * c:8 * c + 8], 16.0,
+           8.0 * (c % 2), A.mult, A.add)
+    op("v", ["a8"], ["a127"], V.tensor_scalar, T.a127[:], T.a8[:], -127.0, None, A.mult)
+    op("v", ["taui"], ["tau"], V.tensor_scalar, T.tau[:], T.taui[:], -1.0, 0.5, A.mult, A.add)
+    op("v", ["a127"] + ["a16_%d" % c for c in range(4)], ["asum"], V.tensor_tensor, T.asum[:], T.a127[:], T.a16[:],
+       A.add)
+    for b in range(4):
+        op("v", ["b0", "offb"], ["bh%d" % b], V.tensor_scalar, T.bh[:, 144 * b:144 * b + 128],
+           T.b0[:, 0:512].indirect(T.offb[:, 8 * b:8 * b + 8]), 0.5, None, A.mult)
+        if b == 0:
+            op("v", ["asum"], ["offa"], V.tensor_copy, T.offa[:], T.asum[:])
+
+    def x_parts(h):
+        for b in range(4):
+            o = 512 * b + 256 * h
+            op("s", ["xs", "offx%d" % b], ["xh%d_%d" % (b, h)], S.activation, T.xh[:, o:o + 256],
+               T.xs[:, 0:1024].indirect(T.offx[:, 32 * b + 16 * h:32 * b + 16 * h + 16]), ACT.Copy, scale=0.5)
+
+    def counting_constants():
+        op("v", ["ci", "pf"], ["ct"], V.tensor_scalar, T.ct[:], T.ci[:], pf(0), 1024.0, A.is_equal, A.mult)
+        op("v", ["jrow", "pc4"], ["cb"], V.tensor_scalar, T.cb[:], T.jrow[:, 0:8], 1024.0, pc(4), A.mult, A.add)
+        op("v", ["ct"], ["qc"], V.quantize_mx, T.qc[:], T.sc[:], T.ct[:])
+
+    def unpacking_constants(step):
+        if step == 0:
+            for b in range(4):
+                op("v", ["jrow", "pf", "et"], ["et%d" % b], V.tensor_scalar, T.et[:, 512 * b + b:512 * b + 512:4],
+                   T.jrow[:], pf(4), None, A.is_equal)
+        else:
+            op("v", ["et%d" % b for b in range(4)], ["qe"], V.quantize_mx, T.qe[:], T.se[:], T.et[:])
+
+    def output_constants():
+        op("v", ["jrow", "pc3"], ["offn"], V.tensor_scalar, T.offn[:], T.jrow[:, 0:16:2], pc(3), None, A.add)
+        op("v", ["pc3"], ["pc7"], V.tensor_scalar, pc(7), pc(3), 4.0, None, A.mult)
+        op("v", ["vs"], ["qv"], V.quantize_mx, T.qv[:], T.sv[:], T.vs[:])
+        op("v", ["pat2", "pc7"], ["offm"], V.tensor_scalar, T.offm[:], T.pat[:, 32:64], pc(7), None, A.add)
+        op("v", [], ["base"], V.memset, T.base[:, 0:64], float(64 * ((rank - ROUNDS) % n_ranks)))
+        op("v", [], ["base2"], V.memset, T.base[:, 64:128], float(64 * ((rank + ROUNDS) % n_ranks)))
+
+    four = [(f, h) for f in range(2) for h in range(2)]
+    for t in range(ROUNDS):
+        last = t == ROUNDS - 1
+        qzy, szy, qin, sin, lst, lin = [T[k + str(t)] for k in ("qzy", "szy", "qin", "sin", "lst", "lin")]
+
+        def scorers():
+            for b in range(4):
+                op("s", ["bh%d" % b, "offs0", "offs1"], ["st%d" % b], S.activation, T.st[:, b:1024:4],
+                   T.bh[:, 144 * b:144 * b + 144].indirect(T.offs[:, 0:16]), ACT.Copy, scale=2.0)
+
+        def candidates(h):
+            for b in range(4):
+                o = 512 * b + 256 * h
+                op("v", ["bh%d" % b, "xh%d_%d" % (b, h), "offa"], ["zy%d_%d" % (b, h)], V.tensor_tensor,
+                   T.zy[:, 1024 * h + b:1024 * h + 1024:4],
+                   T.bh[:, 144 * b:144 * b + 128].indirect(T.offa[:, 16 * h:16 * h + 16]), T.xh[:, o:o + 256], A.add)
+
+        def scores(h):
+            for f in range(2):
+                c, o = 256 * f + 128 * h, 1024 * h + 512 * f
+                op("v", ["zy%d_%d" % (b, h) for b in range(4)], ["qzy%d_%d" % (f, h)], V.quantize_mx, qzy[:, c:c + 128],
+                   szy[:, c:c + 128], T.zy[:, o:o + 512])
+            if h == 0:
+                op("v", ["st%d" % b for b in range(4)], ["qs"], V.quantize_mx, T.qs[:], T.ss[:], T.st[:])
+            for f in range(2):
+                c = 256 * f + 128 * h
+                op("p", ["qs", "qzy%d_%d" % (f, h)], ["pss%d" % h], P.matmul_mx, T.pss[:, 512 * h:512 * h + 128],
+                   T.qs[:, 128 * f:128 * f + 128], T.ss[:, 128 * f:128 * f + 128], qzy[:, c:c + 128], szy[:, c:c + 128],
+                   f == 0, f == 1)
+
+        def rows(h):
+            op("s", [], ["pss%d" % h, "rows%d" % h], S.activation, T.rows[:, 128 * h:128 * h + 128],
+               T.pss[:, 512 * h:512 * h + 128], ACT.Copy)
+            op("s", ["rows%d" % h, "offp"], ["piv%d" % h], S.activation, T.piv[:, 16 * h:16 * h + 16],
+               T.rows[:, 128 * h:128 * h + 128].indirect(T.offp[:, 0:1]), ACT.Copy)
+
+        def origins(q):
+            src = T.org[:, 0:128].indirect(T.offa[:, 0:32])
+            if q == "v":
+                op("v", ["org", "offa"], ["ozy"], V.tensor_copy, T.ozy[:], src)
+            else:
+                op("s", ["org", "offa"], ["ozy"], S.activation, T.ozy[:], src, ACT.Copy)
+            dmas("y", "oa%d" % t, ["ozy"], ["oout"],
+                 [(T.oout[2 * t + f, 64 * h:64 * h + 64, :], T.ozy[0:128:16, 256 * h + 128 * f:256 * h + 128 * f + 128])
+                  for f, h in four])
+
+        def land_origins():
+            dmas("y", "ob%d" % t, ["oland"], ["oin"],
+                 [(T.oin[0:128:16, 256 * f + 128 * h:256 * f + 128 * h + 128], T.oland[2 * t + f, 64 * h:64 * h + 64, :])
+                  for f, h in four])
+
+        def lane(q, lo, hi, b):
+            return ["sig%d_%d_%d" % (q, k, b) for k in range(lo, hi)]
+
+        def blocks(q, lo, hi):
+            return [k for b in range(4) for k in lane(q, lo, hi, b)]
+
+        def seen(q, lo, hi):
+            return ["piv%d" % (q // 4)] + ["rows%d" % h for h in range(lo // 4, (hi - 1) // 4 + 1)]
+
+        def signs(q, lo, hi):
+            for b in range(4):
+                op("s", seen(q, lo, hi), lane(q, lo, hi, b), S.activation,
+                   T.sig[:, 1024 * q + 128 * lo + b:1024 * q + 128 * hi:4], T.rows[:, 32 * lo:32 * hi], ACT.Sign,
+                   bias=T.piv[:, 4 * q + b:4 * q + b + 1], scale=-1.0)
+
+        def direct(q, lo, hi):
+            for b in range(4):
+                op("v", seen(q, lo, hi), lane(q, lo, hi, b), V.tensor_scalar,
+                   T.sig[:, 1024 * q + 128 * lo + b:1024 * q + 128 * hi:4], T.rows[:, 32 * lo:32 * hi],
+                   T.piv[:, 4 * q + b:4 * q + b + 1], None, A.is_le if lo > q else A.is_lt)
+
+        def decide(q, lo, hi):
+            if lo <= q < hi:
+                v = T.sig[:, 1152 * q:1152 * q + 128]
+                op("v", ["tau"], blocks(q, q, q + 1), V.tensor_tensor, v, v, T.tau[:], A.is_gt)
+            for a, b, how in ((lo, min(hi, q), A.is_gt), (max(lo, q + 1), hi, A.is_ge)):
+                if a < b:
+                    v = T.sig[:, 1024 * q + 128 * a:1024 * q + 128 * b]
+                    op("v", [], blocks(q, a, b), V.tensor_scalar, v, v, 0.0, None, how)
+
+        done = []
+
+        def count(q):
+            op("v", blocks(q, 0, 8), ["qg%d" % q], V.quantize_mx, T.qg[:, 256 * q:256 * q + 256],
+               T.sg[:, 256 * q:256 * q + 256], T.sig[:, 1024 * q:1024 * q + 1024])
+            op("p", ["qc", "qg%d" % q], ["psr"], P.matmul_mx, T.psr[:, 0:256], T.qc[:], T.sc[:],
+               T.qg[:, 256 * q:256 * q + 256], T.sg[:, 256 * q:256 * q + 256], len(done) == 0, len(done) == 7)
+            done.append(q)
+            if len(done) == CFG["unpack"]:
+                for b in range(4):
+                    op("p", ["qe", "qin"], ["psd%d" % b], P.matmul_mx, T.psd[:, 512 * b:512 * b + 512],
+                       T.qe[:, 128 * b:128 * b + 128], T.se[:, 128 * b:128 * b + 128], qin[:], sin[:], True, True)
+
+        if t == 0:
+            x_parts(0)
+        scorers()
+        if t == 0:
+            x_parts(1)
+        else:
+            origins("s")
+        candidates(0)
+        if t == 0:
+            counting_constants()
+        scores(0)
+        candidates(1)
+        rows(0)
+        for q in range(CFG["early"]):
+            signs(q, 0, 4)
+        scores(1)
+        send("ac%d" % t, ["qzy%d_%d" % fh for fh in four], "qin", (u8(qzy[:, 0:256]), u8(qin[:, 0:256])),
+             (u8(qzy[:, 256:512]), u8(qin[:, 256:512])))
+        send("ac%d" % t, [], "qin", (szy[:, 0:256], sin[:, 0:256]), (szy[:, 256:512], sin[:, 256:512]))
+        if t == 0:
+            op("g", [], ["ones"], g.iota, T.ones[:], [[0, 1024]], 1, 0, **small)
+            origins("v")
+        send("ao%d" % t, ["oout"], "oland", (T.oout[2 * t], T.oland[2 * t]), (T.oout[2 * t + 1], T.oland[2 * t + 1]))
+        rows(1)
+        for step, q, lo, hi in PLAN:
+            if step == "count":
+                count(q)
+                if t == 0 and len(done) <= 2:
+                    unpacking_constants(len(done) - 1)
+                if len(done) == 1:
+                    land_origins()
+            else:
+                {"signs": signs, "direct": direct, "decide": decide}[step](q, lo, hi)
+        op("v", [], ["psr", "rk"], V.tensor_copy, T.rk[:], T.psr[:, 0:256])
+        for n in range(8):
+            v = T.dif[:, 256 * n:256 * n + 256]
+            if n < 8 - CFG["ns"]:
+                op("v", ["rk", "cb"], ["dif%d" % n], V.tensor_scalar, v, T.rk[:], T.cb[:, n:n + 1], 1024.0,
+                   A.not_equal, A.mult)
+            else:
+                op("s", ["rk", "cb"], ["dif%d" % n], S.activation, v, T.rk[:], ACT.Abs, bias=T.cb[:, n:n + 1],
+                   scale=-1.0)
+        cuts = CFG["cuts"]
+        for lo, hi in zip(cuts, cuts[1:]):
+            op("v", ["ones"] + ["dif%d" % n for n in range(lo, hi)], ["run%d" % lo], V.tensor_tensor_scan,
+               T.run[:, 256 * lo:256 * hi], T.dif[:, 256 * lo:256 * hi], T.ones[:, 0:256 * (hi - lo)], 0.0,
+               A.min, A.add)
+        runs = ["run%d" % n for n in cuts[:-1]]
+        ends = T.run[:, 255:2048:256]
+        op("v", runs + ["pc12", "pc13"], ["lsta"], V.tensor_scalar, lst[:, 0:8], ends, pc(12), pc(13), A.mult, A.add)
+        op("v", runs + ["pc14", "pc6"], ["lstb"], V.tensor_scalar, lst[:, 8:16], ends, pc(14), pc(6), A.mult, A.add)
+        send("al%d" % t, ["lsta", "lstb"], "lin", (lst[:, 0:8], lin[:, 0:8]), (lst[:, 8:16], lin[:, 8:16]))
+        for b in range(4):
+            out, src = T.dp[:, 512 * b:512 * b + 512], T.psd[:, 512 * b:512 * b + 512]
+            if b < 2:
+                op("v", [], ["psd%d" % b, "dp%d" % b], V.tensor_copy, out, src)
+            else:
+                op("s", [], ["psd%d" % b, "dp%d" % b], S.activation, out, src, ACT.Copy)
+        if t == 0:
+            output_constants()
+        op("v", ["lin"], ["lsum"], V.tensor_tensor, T.lsum[:], lin[:, 0:8], lin[:, 8:16], A.add)
+        op("v", ["lsum", "pc6"], ["offf"], V.tensor_scalar, T.offf[:], T.lsum[:], pc(6), None, A.add)
+        for b in range(4):
+            out, src = T.ft[:, b:512:4], T.dp[:, 512 * b:512 * b + 512].indirect(T.offf[:, 0:8])
+            if b < 2:
+                op("v", ["dp%d" % b, "offf"], ["ft%d" % b], V.tensor_copy, out, src)
+            else:
+                op("s", ["dp%d" % b, "offf"], ["ft%d" % b], S.activation, out, src, ACT.Copy)
+        fts = ["ft%d" % b for b in range(4)]
+        op("v", fts, ["qf"], V.quantize_mx, T.qf[:], T.sf[:], T.ft[:])
+        op("s", ["oin", "offf"], ["org"], S.activation, T.org[:], T.oin[:, 0:512].indirect(T.offf[:, 0:8]), ACT.Copy)
+        if last:
+            op("v", fts + ["offm"], ["fh"], V.tensor_copy, T.fh[:], T.ft[:, 0:512].indirect(T.offm[:, 0:32]))
+        else:
+            op("v", fts, ["fh"], V.tensor_scalar, T.fh[:], T.ft[:], 0.5, None, A.mult)
+        for b in range(4):
+            op("p", ["qw", "qf"], ["psd%d" % b], P.matmul_mx, T.psd[:, 512 * b:512 * b + 128],
+               T.qw[:, 128 * b:128 * b + 128], T.sw[:, 128 * b:128 * b + 128], T.qf[:], T.sf[:], True, True)
+        for b in range(4):
+            rl = T.rl[:, 128 * b:128 * b + 128]
+            op("s", [], ["psd%d" % b, "rl%d" % b], S.activation, rl, T.psd[:, 512 * b:512 * b + 128], ACT.Relu,
+               scale=0.03125 if last else 0.015625)
+            if last:
+                op("v", ["rl%d" % b, "fh", "offn"], ["bt%d" % b], V.tensor_tensor, T.bt[:, b:512:4],
+                   rl.indirect(T.offn[:, 0:8]), T.fh[:, 128 * b:128 * b + 128], A.add)
+            else:
+                op("v", ["rl%d" % b, "fh"], ["bh%d" % b], V.tensor_tensor, T.bh[:, 144 * b:144 * b + 128], rl,
+                   T.fh[:, b:512:4], A.add)
+
+    op("v", ["bt%d" % b for b in range(4)], ["qb"], V.quantize_mx, T.qb[:], T.sb[:], T.bt[:])
+    op("p", ["qv", "qb"], ["pss0"], P.matmul_mx, T.pss[:, 0:128], T.qv[:], T.sv[:], T.qb[:], T.sb[:], True, True)
+    op("v", ["org", "offn", "base", "base2"], ["otb"], V.tensor_tensor, T.otb[:],
+       T.org[:, 0:128].indirect(T.offn[:, 0:8]), T.base[:], A.add)
+    dmas("y", "stc", ["qb"], [], [(T.oc[:], u8(T.qb[:]))] +
+         [(T.osc[4 * k:4 * k + 4, :], T.sb[32 * k:32 * k + 4, :]) for k in range(4)])
+    op("s", [], ["pss0", "yb"], S.activation, T.yb[:], T.pss[:, 0:128], ACT.Copy)
+    dmas("s", "sty", ["yb"], [], [(T.y[:], T.yb[:])])
+    dmas("y", "sto", ["otb"], [], [(T.ot[:], T.otb[0:128:16, :])])
+    for sem, val in total.items():
+        g.wait_ge(T.sem[sem], val)

@@ -1,12 +1,14 @@
 from concourse.bass import DstId, RemoteDMATransfer
-from concourse.mybir import dt, AluOpType, AxisListType, ActivationFunctionType
+from concourse.mybir import dt, AluOpType, ActivationFunctionType
 
 ROUNDS = 3
 CFG = {"ns": 4, "cuts": [0, 4, 8], "unpack": 3, "early": 2}
-_SIGNED = [(3, 0), (4, 0), (7, 0), (6, 0), (5, 0), (2, 0), (1, 4)]
-PLAN = ([("decide", 0, 0, 4), ("decide", 1, 0, 4)] + [("signs", q, lo, 8) for q, lo in _SIGNED] +
-        [("direct", 0, 4, 8), ("count", 0, 0, 0)] +
-        [(step, q, lo, 8) for q, lo in _SIGNED for step in ("decide", "count")])
+PLAN = ([("decide", 0, 0, 4), ("decide", 1, 0, 4)] + [("signs", q, 0, 8) for q in (3, 4, 5, 2, 6, 7)] +
+        [("relu", 7, 0, 5), ("origins", 0, 0, 0),
+         ("direct", 0, 4, 8), ("decide", 3, 0, 8), ("count", 0, 0, 0), ("direct", 1, 4, 8), ("count", 3, 0, 0),
+         ("decide", 4, 0, 8), ("count", 1, 0, 0), ("decide", 5, 0, 8), ("count", 4, 0, 0), ("decide", 2, 0, 8),
+         ("count", 5, 0, 0), ("decide", 6, 0, 8), ("count", 2, 0, 0), ("decide", 7, 5, 8), ("count", 6, 0, 0),
+         ("count", 7, 0, 0)])
 X4, U8, BF, F32, I32, U16 = "float8_e4m3fn_x4", "uint8", "bfloat16", "float32", "int32", "uint16"
 
 
@@ -117,9 +119,9 @@ def rank_program(g, core, T, topo):
         return [(out[:, 16 * h + 8 * f:16 * h + 8 * f + 8], (left, right)[f][:, 8 * h:8 * h + 8])
                 for h in range(2) for f in range(2)]
 
-    dmas("s", "ldx", [], ["xs"], [(T.xs[:], T.x[:])])
-    dmas("y", "ldlx", [], ["lxb"], halves(T.lxb, T.lx, T.rx))
     dmas("s", "ldb", [], ["b0"], [(T.b0[:, 0:256], T.l0[:]), (T.b0[:, 256:512], T.r0[:])])
+    dmas("y", "ldlx", [], ["lxb"], halves(T.lxb, T.lx, T.rx))
+    dmas("s", "ldx", [], ["xs"], [(T.xs[:], T.x[:])])
     dmas("y", "ldla", [], ["lab"], halves(T.lab, T.la, T.ra))
     dmas("y", "ldw", [], ["qw"], [(u8(T.qw[:]), T.wc[:]), (T.sw[:], T.ws[:])])
     dmas("y", "ldv", [], ["vs"], [(T.vs[:], T.v[:])])
@@ -129,11 +131,14 @@ def rank_program(g, core, T, topo):
     op("g", [], ["pat"], g.iota, T.pat[:, 0:32], [[1, 4], [4, 8]], 0, 0, **small)
     op("g", [], ["taui"], g.iota, T.taui[:], [[1, 32], [-8, 4]], 0, 0, **small)
     op("g", [], ["jrow"], g.iota, T.jrow[:], [[1, 128]], 0, 0, **small)
-    op("g", [], ["org"], g.iota, T.org[:], [[1, 8], [0, 2], [8, 8]], 0, 0, **small)
     op("g", [], ["ci"], g.iota, T.ci[:], [[1, 8], [8, 2], [0, 32]], 0, 0, **small)
+    op("g", [], ["org"], g.iota, T.org[:], [[1, 8], [0, 2], [8, 8]], 0, 0, **small)
     op("g", [], ["pat2"], g.iota, T.pat[:, 32:64], [[1, 4], [8, 8]], 0, 0, **small)
+    op("g", [], ["ones"], g.iota, T.ones[:], [[0, 1024]], 1, 0, **small)
     op("g", [], ["oin"], g.iota, T.oin[:], [[0, 512]], 0, 0, **small)
-    op("g", [], ["et"], g.iota, T.et[:], [[0, 2048]], 0, 0, **small)
+    for b in range(4):
+        op("g", ["ones"], ["et%d" % b], g.affine_select, T.et[:, 512 * b:512 * b + 512], T.ones[:, 0:512],
+           [[8, 128], [1, 4]], A.is_equal, 0.0, -b, -8)
 
     def pf(c):
         return T.pf[:, c:c + 1]
@@ -143,10 +148,10 @@ def rank_program(g, core, T, topo):
 
     planes = ["bh%d" % b for b in range(4)]
     op("v", [], planes, V.memset, T.bh[:], 0.0)
-    for c, (sh, m) in enumerate(((0, 15), (4, 7), (0, 7), (3, 1), (0, 127))):
+    for c, (sh, m) in enumerate(((0, 15), (4, 7), (0, 7), (3, 1))):
         op("v", ["pint"], ["pb%d" % c], V.tensor_scalar, T.pb[:, c:c + 1], T.pint[:], sh, m,
            A.logical_shift_right, A.bitwise_and)
-    op("v", ["pb%d" % c for c in range(5)], ["pf"], V.tensor_copy, T.pf[:, 0:5], T.pb[:, 0:5])
+    op("v", ["pb%d" % c for c in range(4)], ["pf"], V.tensor_copy, T.pf[:, 0:4], T.pb[:, 0:4])
     for c, a, m, b in ((0, 0, 32.0, 0.0), (2, 0, 8.0, pf(1)), (3, 2, 16.0, pf(3)), (4, 2, 8192.0, 0.0),
                        (6, 3, 256.0, 0.0), (8, 3, 128.0, 0.0), (9, 3, -128.0, 128.0), (10, 0, 1.0, 8.0),
                        (11, 0, 1.0, -8.0), (12, 3, 1.0, -1.0), (13, 3, -256.0, 256.0), (14, 3, -1.0, 0.0)):
@@ -158,6 +163,9 @@ def rank_program(g, core, T, topo):
     op("v", ["pc2"], ["offp"], V.tensor_copy, T.offp[:, 0:1], pc(2))
     op("v", ["taui", "pf"], ["taui"], V.tensor_scalar, T.taui[:], T.taui[:], pf(1), 0.0, A.subtract, A.is_gt)
     for b in range(4):
+        op("v", ["b0", "offb"], ["bh%d" % b], V.tensor_scalar, T.bh[:, 144 * b:144 * b + 128],
+           T.b0[:, 0:512].indirect(T.offb[:, 8 * b:8 * b + 8]), 0.5, None, A.mult)
+    for b in range(4):
         op("v", ["lxb"], ["offx%d" % b], V.tensor_scalar, T.offx[:, 32 * b:32 * b + 32], T.lxb[:], 4.0, float(b),
            A.mult, A.add)
     op("v", ["lab"], ["a8"], V.tensor_scalar, T.a8[:], T.lab[:], 3, None, A.logical_shift_right)
@@ -168,30 +176,16 @@ def rank_program(g, core, T, topo):
     op("v", ["taui"], ["tau"], V.tensor_scalar, T.tau[:], T.taui[:], -1.0, 0.5, A.mult, A.add)
     op("v", ["a127"] + ["a16_%d" % c for c in range(4)], ["asum"], V.tensor_tensor, T.asum[:], T.a127[:], T.a16[:],
        A.add)
-    for b in range(4):
-        op("v", ["b0", "offb"], ["bh%d" % b], V.tensor_scalar, T.bh[:, 144 * b:144 * b + 128],
-           T.b0[:, 0:512].indirect(T.offb[:, 8 * b:8 * b + 8]), 0.5, None, A.mult)
-        if b == 0:
-            op("v", ["asum"], ["offa"], V.tensor_copy, T.offa[:], T.asum[:])
+    op("v", ["ci", "pf"], ["ct"], V.tensor_scalar, T.ct[:], T.ci[:], pf(0), 1024.0, A.is_equal, A.mult)
+    op("v", ["asum"], ["offa"], V.tensor_copy, T.offa[:], T.asum[:])
+    op("v", ["jrow", "pc4"], ["cb"], V.tensor_scalar, T.cb[:], T.jrow[:, 0:8], 1024.0, pc(4), A.mult, A.add)
+    op("v", ["ct"], ["qc"], V.quantize_mx, T.qc[:], T.sc[:], T.ct[:])
 
     def x_parts(h):
         for b in range(4):
             o = 512 * b + 256 * h
             op("s", ["xs", "offx%d" % b], ["xh%d_%d" % (b, h)], S.activation, T.xh[:, o:o + 256],
                T.xs[:, 0:1024].indirect(T.offx[:, 32 * b + 16 * h:32 * b + 16 * h + 16]), ACT.Copy, scale=0.5)
-
-    def counting_constants():
-        op("v", ["ci", "pf"], ["ct"], V.tensor_scalar, T.ct[:], T.ci[:], pf(0), 1024.0, A.is_equal, A.mult)
-        op("v", ["jrow", "pc4"], ["cb"], V.tensor_scalar, T.cb[:], T.jrow[:, 0:8], 1024.0, pc(4), A.mult, A.add)
-        op("v", ["ct"], ["qc"], V.quantize_mx, T.qc[:], T.sc[:], T.ct[:])
-
-    def unpacking_constants(step):
-        if step == 0:
-            for b in range(4):
-                op("v", ["jrow", "pf", "et"], ["et%d" % b], V.tensor_scalar, T.et[:, 512 * b + b:512 * b + 512:4],
-                   T.jrow[:], pf(4), None, A.is_equal)
-        else:
-            op("v", ["et%d" % b for b in range(4)], ["qe"], V.quantize_mx, T.qe[:], T.se[:], T.et[:])
 
     def output_constants():
         op("v", ["jrow", "pc3"], ["offn"], V.tensor_scalar, T.offn[:], T.jrow[:, 0:16:2], pc(3), None, A.add)
@@ -200,6 +194,9 @@ def rank_program(g, core, T, topo):
         op("v", ["pat2", "pc7"], ["offm"], V.tensor_scalar, T.offm[:], T.pat[:, 32:64], pc(7), None, A.add)
         op("v", [], ["base"], V.memset, T.base[:, 0:64], float(64 * ((rank - ROUNDS) % n_ranks)))
         op("v", [], ["base2"], V.memset, T.base[:, 64:128], float(64 * ((rank + ROUNDS) % n_ranks)))
+
+    def picked_origins():
+        op("s", ["oin", "offf"], ["org"], S.activation, T.org[:], T.oin[:, 0:512].indirect(T.offf[:, 0:8]), ACT.Copy)
 
     four = [(f, h) for f in range(2) for h in range(2)]
     for t in range(ROUNDS):
@@ -219,12 +216,12 @@ def rank_program(g, core, T, topo):
                    T.bh[:, 144 * b:144 * b + 128].indirect(T.offa[:, 16 * h:16 * h + 16]), T.xh[:, o:o + 256], A.add)
 
         def scores(h):
+            if h == 0:
+                op("v", ["st%d" % b for b in range(4)], ["qs"], V.quantize_mx, T.qs[:], T.ss[:], T.st[:])
             for f in range(2):
                 c, o = 256 * f + 128 * h, 1024 * h + 512 * f
                 op("v", ["zy%d_%d" % (b, h) for b in range(4)], ["qzy%d_%d" % (f, h)], V.quantize_mx, qzy[:, c:c + 128],
                    szy[:, c:c + 128], T.zy[:, o:o + 512])
-            if h == 0:
-                op("v", ["st%d" % b for b in range(4)], ["qs"], V.quantize_mx, T.qs[:], T.ss[:], T.st[:])
             for f in range(2):
                 c = 256 * f + 128 * h
                 op("p", ["qs", "qzy%d_%d" % (f, h)], ["pss%d" % h], P.matmul_mx, T.pss[:, 512 * h:512 * h + 128],
@@ -237,17 +234,18 @@ def rank_program(g, core, T, topo):
             op("s", ["rows%d" % h, "offp"], ["piv%d" % h], S.activation, T.piv[:, 16 * h:16 * h + 16],
                T.rows[:, 128 * h:128 * h + 128].indirect(T.offp[:, 0:1]), ACT.Copy)
 
-        def origins(q):
-            src = T.org[:, 0:128].indirect(T.offa[:, 0:32])
-            if q == "v":
-                op("v", ["org", "offa"], ["ozy"], V.tensor_copy, T.ozy[:], src)
-            else:
-                op("s", ["org", "offa"], ["ozy"], S.activation, T.ozy[:], src, ACT.Copy)
+        def origins():
+            if t > 0:
+                picked_origins()
+            op("s", ["org", "offa"], ["ozy"], S.activation, T.ozy[:], T.org[:, 0:128].indirect(T.offa[:, 0:32]),
+               ACT.Copy)
             dmas("y", "oa%d" % t, ["ozy"], ["oout"],
                  [(T.oout[2 * t + f, 64 * h:64 * h + 64, :], T.ozy[0:128:16, 256 * h + 128 * f:256 * h + 128 * f + 128])
                   for f, h in four])
 
-        def land_origins():
+        def move_origins():
+            send("ao%d" % t, ["oout"], "oland", (T.oout[2 * t], T.oland[2 * t]),
+                 (T.oout[2 * t + 1], T.oland[2 * t + 1]))
             dmas("y", "ob%d" % t, ["oland"], ["oin"],
                  [(T.oin[0:128:16, 256 * f + 128 * h:256 * f + 128 * h + 128], T.oland[2 * t + f, 64 * h:64 * h + 64, :])
                   for f, h in four])
@@ -282,6 +280,10 @@ def rank_program(g, core, T, topo):
                     v = T.sig[:, 1024 * q + 128 * a:1024 * q + 128 * b]
                     op("v", [], blocks(q, a, b), V.tensor_scalar, v, v, 0.0, None, how)
 
+        def relu(q, lo, hi):
+            v = T.sig[:, 1024 * q + 128 * lo:1024 * q + 128 * hi]
+            op("s", [], blocks(q, lo, hi), S.activation, v, v, ACT.Relu)
+
         done = []
 
         def count(q):
@@ -290,21 +292,20 @@ def rank_program(g, core, T, topo):
             op("p", ["qc", "qg%d" % q], ["psr"], P.matmul_mx, T.psr[:, 0:256], T.qc[:], T.sc[:],
                T.qg[:, 256 * q:256 * q + 256], T.sg[:, 256 * q:256 * q + 256], len(done) == 0, len(done) == 7)
             done.append(q)
+            if t == 0 and len(done) == CFG["unpack"] - 1:
+                op("v", ["et%d" % b for b in range(4)], ["qe"], V.quantize_mx, T.qe[:], T.se[:], T.et[:])
             if len(done) == CFG["unpack"]:
                 for b in range(4):
                     op("p", ["qe", "qin"], ["psd%d" % b], P.matmul_mx, T.psd[:, 512 * b:512 * b + 512],
                        T.qe[:, 128 * b:128 * b + 128], T.se[:, 128 * b:128 * b + 128], qin[:], sin[:], True, True)
 
-        if t == 0:
-            x_parts(0)
         scorers()
         if t == 0:
+            x_parts(0)
             x_parts(1)
-        else:
-            origins("s")
+        if last:
+            origins()
         candidates(0)
-        if t == 0:
-            counting_constants()
         scores(0)
         candidates(1)
         rows(0)
@@ -314,20 +315,18 @@ def rank_program(g, core, T, topo):
         send("ac%d" % t, ["qzy%d_%d" % fh for fh in four], "qin", (u8(qzy[:, 0:256]), u8(qin[:, 0:256])),
              (u8(qzy[:, 256:512]), u8(qin[:, 256:512])))
         send("ac%d" % t, [], "qin", (szy[:, 0:256], sin[:, 0:256]), (szy[:, 256:512], sin[:, 256:512]))
-        if t == 0:
-            op("g", [], ["ones"], g.iota, T.ones[:], [[0, 1024]], 1, 0, **small)
-            origins("v")
-        send("ao%d" % t, ["oout"], "oland", (T.oout[2 * t], T.oland[2 * t]), (T.oout[2 * t + 1], T.oland[2 * t + 1]))
+        if last:
+            move_origins()
         rows(1)
         for step, q, lo, hi in PLAN:
             if step == "count":
                 count(q)
-                if t == 0 and len(done) <= 2:
-                    unpacking_constants(len(done) - 1)
-                if len(done) == 1:
-                    land_origins()
+            elif step == "origins":
+                if 0 < t < ROUNDS - 1:
+                    origins()
+                    move_origins()
             else:
-                {"signs": signs, "direct": direct, "decide": decide}[step](q, lo, hi)
+                {"signs": signs, "direct": direct, "decide": decide, "relu": relu}[step](q, lo, hi)
         op("v", [], ["psr", "rk"], V.tensor_copy, T.rk[:], T.psr[:, 0:256])
         for n in range(8):
             v = T.dif[:, 256 * n:256 * n + 256]
@@ -354,6 +353,8 @@ def rank_program(g, core, T, topo):
             else:
                 op("s", [], ["psd%d" % b, "dp%d" % b], S.activation, out, src, ACT.Copy)
         if t == 0:
+            origins()
+            move_origins()
             output_constants()
         op("v", ["lin"], ["lsum"], V.tensor_tensor, T.lsum[:], lin[:, 0:8], lin[:, 8:16], A.add)
         op("v", ["lsum", "pc6"], ["offf"], V.tensor_scalar, T.offf[:], T.lsum[:], pc(6), None, A.add)
@@ -365,9 +366,10 @@ def rank_program(g, core, T, topo):
                 op("s", ["dp%d" % b, "offf"], ["ft%d" % b], S.activation, out, src, ACT.Copy)
         fts = ["ft%d" % b for b in range(4)]
         op("v", fts, ["qf"], V.quantize_mx, T.qf[:], T.sf[:], T.ft[:])
-        op("s", ["oin", "offf"], ["org"], S.activation, T.org[:], T.oin[:, 0:512].indirect(T.offf[:, 0:8]), ACT.Copy)
         if last:
-            op("v", fts + ["offm"], ["fh"], V.tensor_copy, T.fh[:], T.ft[:, 0:512].indirect(T.offm[:, 0:32]))
+            op("s", fts + ["offm", "fh"], ["fh3"], S.activation, T.fh[:, 384:512],
+               T.ft[:, 0:512].indirect(T.offm[:, 24:32]), ACT.Copy)
+            op("v", fts + ["offm"], ["fh"], V.tensor_copy, T.fh[:, 0:384], T.ft[:, 0:512].indirect(T.offm[:, 0:24]))
         else:
             op("v", fts, ["fh"], V.tensor_scalar, T.fh[:], T.ft[:], 0.5, None, A.mult)
         for b in range(4):
@@ -378,12 +380,13 @@ def rank_program(g, core, T, topo):
             op("s", [], ["psd%d" % b, "rl%d" % b], S.activation, rl, T.psd[:, 512 * b:512 * b + 128], ACT.Relu,
                scale=0.03125 if last else 0.015625)
             if last:
-                op("v", ["rl%d" % b, "fh", "offn"], ["bt%d" % b], V.tensor_tensor, T.bt[:, b:512:4],
+                op("v", ["rl%d" % b, "fh", "fh3", "offn"], ["bt%d" % b], V.tensor_tensor, T.bt[:, b:512:4],
                    rl.indirect(T.offn[:, 0:8]), T.fh[:, 128 * b:128 * b + 128], A.add)
             else:
                 op("v", ["rl%d" % b, "fh"], ["bh%d" % b], V.tensor_tensor, T.bh[:, 144 * b:144 * b + 128], rl,
                    T.fh[:, b:512:4], A.add)
 
+    picked_origins()
     op("v", ["bt%d" % b for b in range(4)], ["qb"], V.quantize_mx, T.qb[:], T.sb[:], T.bt[:])
     op("p", ["qv", "qb"], ["pss0"], P.matmul_mx, T.pss[:, 0:128], T.qv[:], T.sv[:], T.qb[:], T.sb[:], True, True)
     op("v", ["org", "offn", "base", "base2"], ["otb"], V.tensor_tensor, T.otb[:],

from concourse.bass import DstId, RemoteDMATransfer
from concourse.mybir import dt, AluOpType, ActivationFunctionType

ROUNDS = 3
CFG = {"ns": 4, "cuts": [0, 4, 8], "unpack": 3, "early": 2}
PLAN = ([("decide", 0, 0, 4), ("decide", 1, 0, 4)] + [("signs", q, 0, 8) for q in (3, 4, 5, 2, 6, 7)] +
        [("relu", 7, 0, 5), ("origins", 0, 0, 0),
         ("direct", 0, 4, 8), ("decide", 3, 0, 8), ("count", 0, 0, 0), ("direct", 1, 4, 8), ("count", 3, 0, 0),
         ("decide", 4, 0, 8), ("count", 1, 0, 0), ("decide", 5, 0, 8), ("count", 4, 0, 0), ("decide", 2, 0, 8),
         ("count", 5, 0, 0), ("decide", 6, 0, 8), ("count", 2, 0, 0), ("decide", 7, 5, 8), ("count", 6, 0, 0),
         ("count", 7, 0, 0)])
X4, U8, BF, F32, I32, U16 = "float8_e4m3fn_x4", "uint8", "bfloat16", "float32", "int32", "uint16"


def _sb(n, d):
    return ("sbuf", [128, n], d)


SCRATCH = {
    "xs": _sb(1024, BF), "b0": _sb(512, BF), "vs": _sb(512, BF), "lab": _sb(32, I32), "lxb": _sb(32, I32),
    "qw": _sb(512, X4), "sw": _sb(512, U8), "qv": _sb(128, X4), "sv": _sb(128, U8),
    "pint": _sb(1, I32), "pb": _sb(8, I32), "pf": _sb(8, F32), "pc": _sb(16, F32),
    "jrow": _sb(128, F32), "pat": _sb(64, F32), "taui": _sb(128, F32), "tau": _sb(128, BF),
    "ci": _sb(512, BF), "ct": _sb(512, BF), "qc": _sb(128, X4), "sc": _sb(128, U8),
    "et": _sb(2048, BF), "qe": _sb(512, X4), "se": _sb(512, U8),
    "cb": _sb(8, F32), "base": _sb(128, F32),
    "a16": _sb(32, F32), "a8": _sb(32, I32), "a127": _sb(32, F32), "asum": _sb(32, F32),
    "offa": _sb(32, U16), "offx": _sb(128, U16), "offb": _sb(32, U16), "offs": _sb(16, U16), "offp": _sb(2, U16),
    "offn": _sb(8, U16), "offm": _sb(32, U16), "offf": _sb(8, U16),
    "xh": _sb(2048, BF), "bh": _sb(576, BF), "zy": _sb(2048, BF), "st": _sb(1024, BF),
    "qs": _sb(256, X4), "ss": _sb(256, U8),
    "rows": _sb(256, F32), "piv": _sb(32, F32), "sig": _sb(8192, BF), "qg": _sb(2048, X4), "sg": _sb(2048, U8),
    "rk": _sb(256, BF), "dif": _sb(2048, BF), "run": _sb(2048, BF), "ones": _sb(1024, BF), "lsum": _sb(8, F32),
    "dp": _sb(2048, BF), "ft": _sb(512, BF), "fh": _sb(512, BF), "qf": _sb(128, X4), "sf": _sb(128, U8),
    "rl": _sb(512, F32), "bt": _sb(512, BF), "qb": _sb(128, X4), "sb": _sb(128, U8), "yb": _sb(128, F32),
    "org": _sb(128, BF), "ozy": _sb(512, BF), "oin": _sb(512, BF), "otb": _sb(128, F32),
    "oout": ("dram", [2 * ROUNDS, 128, 16], BF), "oland": ("dram", [2 * ROUNDS, 128, 16], BF),
    "pss": ("psum", [128, 1024], F32), "psr": ("psum", [128, 512], F32), "psd": ("psum", [128, 2048], F32),
}
SEMAPHORES = ["cv", "cs", "cp", "cg", "sent", "ldx", "ldlx", "ldla", "ldb", "ldw", "ldv", "sty", "sto", "stc"]
for _t in range(ROUNDS):
    SCRATCH["qzy%d" % _t] = _sb(512, X4)
    SCRATCH["szy%d" % _t] = _sb(512, U8)
    SCRATCH["qin%d" % _t] = _sb(512, X4)
    SCRATCH["sin%d" % _t] = _sb(512, U8)
    SCRATCH["lst%d" % _t] = _sb(16, BF)
    SCRATCH["lin%d" % _t] = _sb(16, BF)
    SEMAPHORES += ["ac%d" % _t, "ao%d" % _t, "al%d" % _t, "oa%d" % _t, "ob%d" % _t]


def rank_program(g, core, T, topo):
    rank = T.rank_of(core)
    if rank is None:
        return
    n_ranks = len(T.cores)
    nxt, prv = T.cores[(rank + 1) % n_ranks], T.cores[(rank - 1) % n_ranks]
    A, ACT = AluOpType, ActivationFunctionType
    V, S, P, Y = g.vector, g.scalar, g.tensor, g.sync
    queue = {"v": V, "s": S, "p": P, "g": g, "y": Y}
    total, waited, wrote, read = {}, {}, {}, {}

    def settle(q, r, w):
        need = {}
        toks = [wrote[k] for k in list(r) + list(w) if k in wrote]
        for k in w:
            toks += read.get(k, [])
        for sem, val in toks:
            if not (q == "p" and sem == "cp"):
                need[sem] = max(need.get(sem, 0), val)
        for sem, val in need.items():
            if waited.get((q, sem), 0) < val:
                queue[q].wait_ge(T.sem[sem], val)
                waited[(q, sem)] = val

    def note(tok, r, w):
        for k in r:
            read.setdefault(k, []).append(tok)
        for k in w:
            wrote[k] = tok
            read[k] = []

    def op(q, r, w, fn, *args, **kw):
        settle(q, r, w)
        sem = "c" + q
        total[sem] = total.get(sem, 0) + 1
        fn(*args, **kw).then_inc(T.sem[sem], 1)
        note((sem, total[sem]), r, w)

    def dmas(q, sem, r, w, pairs):
        settle(q, r, w)
        for out, in_ in pairs:
            queue[q].dma_start(out, in_).then_inc(T.sem[sem], 16)
        total[sem] = total.get(sem, 0) + 16 * len(pairs)
        note((sem, total[sem]), r, w)

    def half_mask(dst, upper):
        e = topo.engines(core, dst)
        h = len(e) // 2
        return sum(1 << k for k in (e[h:] if upper else e[:h])), h

    def send(sem, r, arrives, up, down):
        settle("g", r, [])
        ts, n = [], 0
        for dst, (src, land), upper in ((nxt, up, False), (prv, down, True)):
            rid, pid, _ = topo.addr(dst)
            m, h = half_mask(dst, upper)
            n += h
            ts.append(RemoteDMATransfer(dst_ids=[DstId(rid=rid, pnc=pid)], dma_engine_mask=m, remote_sem=T.sem[sem],
                                        src=src, dst=land))
        g.remote_dma_fused(ts, local_sem=T.sem.sent)
        total["sent"] = total.get("sent", 0) + n
        total[sem] = total.get(sem, 0) + n
        wrote[arrives] = (sem, total[sem])

    def u8(view):
        return view.bitcast(dt.uint8)

    def halves(out, left, right):
        return [(out[:, 16 * h + 8 * f:16 * h + 8 * f + 8], (left, right)[f][:, 8 * h:8 * h + 8])
                for h in range(2) for f in range(2)]

    dmas("s", "ldb", [], ["b0"], [(T.b0[:, 0:256], T.l0[:]), (T.b0[:, 256:512], T.r0[:])])
    dmas("y", "ldlx", [], ["lxb"], halves(T.lxb, T.lx, T.rx))
    dmas("s", "ldx", [], ["xs"], [(T.xs[:], T.x[:])])
    dmas("y", "ldla", [], ["lab"], halves(T.lab, T.la, T.ra))
    dmas("y", "ldw", [], ["qw"], [(u8(T.qw[:]), T.wc[:]), (T.sw[:], T.ws[:])])
    dmas("y", "ldv", [], ["vs"], [(T.vs[:], T.v[:])])

    small = dict(allow_small_or_imprecise_dtypes=True)
    op("g", [], ["pint"], g.iota, T.pint[:], [[0, 1]], 0, 1)
    op("g", [], ["pat"], g.iota, T.pat[:, 0:32], [[1, 4], [4, 8]], 0, 0, **small)
    op("g", [], ["taui"], g.iota, T.taui[:], [[1, 32], [-8, 4]], 0, 0, **small)
    op("g", [], ["jrow"], g.iota, T.jrow[:], [[1, 128]], 0, 0, **small)
    op("g", [], ["ci"], g.iota, T.ci[:], [[1, 8], [8, 2], [0, 32]], 0, 0, **small)
    op("g", [], ["org"], g.iota, T.org[:], [[1, 8], [0, 2], [8, 8]], 0, 0, **small)
    op("g", [], ["pat2"], g.iota, T.pat[:, 32:64], [[1, 4], [8, 8]], 0, 0, **small)
    op("g", [], ["ones"], g.iota, T.ones[:], [[0, 1024]], 1, 0, **small)
    op("g", [], ["oin"], g.iota, T.oin[:], [[0, 512]], 0, 0, **small)
    for b in range(4):
        op("g", ["ones"], ["et%d" % b], g.affine_select, T.et[:, 512 * b:512 * b + 512], T.ones[:, 0:512],
           [[8, 128], [1, 4]], A.is_equal, 0.0, -b, -8)

    def pf(c):
        return T.pf[:, c:c + 1]

    def pc(c):
        return T.pc[:, c:c + 1]

    planes = ["bh%d" % b for b in range(4)]
    op("v", [], planes, V.memset, T.bh[:], 0.0)
    for c, (sh, m) in enumerate(((0, 15), (4, 7), (0, 7), (3, 1))):
        op("v", ["pint"], ["pb%d" % c], V.tensor_scalar, T.pb[:, c:c + 1], T.pint[:], sh, m,
           A.logical_shift_right, A.bitwise_and)
    op("v", ["pb%d" % c for c in range(4)], ["pf"], V.tensor_copy, T.pf[:, 0:4], T.pb[:, 0:4])
    for c, a, m, b in ((0, 0, 32.0, 0.0), (2, 0, 8.0, pf(1)), (3, 2, 16.0, pf(3)), (4, 2, 8192.0, 0.0),
                       (6, 3, 256.0, 0.0), (8, 3, 128.0, 0.0), (9, 3, -128.0, 128.0), (10, 0, 1.0, 8.0),
                       (11, 0, 1.0, -8.0), (12, 3, 1.0, -1.0), (13, 3, -256.0, 256.0), (14, 3, -1.0, 0.0)):
        op("v", ["pf"], ["pc%d" % c], V.tensor_scalar, pc(c), pf(a), m, b, A.mult, A.add)
    op("v", ["pat", "pc0"], ["offb"], V.tensor_scalar, T.offb[:], T.pat[:, 0:32], pc(0), None, A.add)
    for c in range(2):
        op("v", planes + ["pc%d" % (8 + c), "pc%d" % (10 + c)], ["offs%d" % c], V.tensor_scalar,
           T.offs[:, 8 * c:8 * c + 8], T.bh[:, 0:8], pc(10 + c), pc(8 + c), A.add, A.max)
    op("v", ["pc2"], ["offp"], V.tensor_copy, T.offp[:, 0:1], pc(2))
    op("v", ["taui", "pf"], ["taui"], V.tensor_scalar, T.taui[:], T.taui[:], pf(1), 0.0, A.subtract, A.is_gt)
    for b in range(4):
        op("v", ["b0", "offb"], ["bh%d" % b], V.tensor_scalar, T.bh[:, 144 * b:144 * b + 128],
           T.b0[:, 0:512].indirect(T.offb[:, 8 * b:8 * b + 8]), 0.5, None, A.mult)
    for b in range(4):
        op("v", ["lxb"], ["offx%d" % b], V.tensor_scalar, T.offx[:, 32 * b:32 * b + 32], T.lxb[:], 4.0, float(b),
           A.mult, A.add)
    op("v", ["lab"], ["a8"], V.tensor_scalar, T.a8[:], T.lab[:], 3, None, A.logical_shift_right)
    for c in range(4):
        op("v", ["lab"], ["a16_%d" % c], V.tensor_scalar, T.a16[:, 8 * c:8 * c + 8], T.lab[:, 8 * c:8 * c + 8], 16.0,
           8.0 * (c % 2), A.mult, A.add)
    op("v", ["a8"], ["a127"], V.tensor_scalar, T.a127[:], T.a8[:], -127.0, None, A.mult)
    op("v", ["taui"], ["tau"], V.tensor_scalar, T.tau[:], T.taui[:], -1.0, 0.5, A.mult, A.add)
    op("v", ["a127"] + ["a16_%d" % c for c in range(4)], ["asum"], V.tensor_tensor, T.asum[:], T.a127[:], T.a16[:],
       A.add)
    op("v", ["ci", "pf"], ["ct"], V.tensor_scalar, T.ct[:], T.ci[:], pf(0), 1024.0, A.is_equal, A.mult)
    op("v", ["asum"], ["offa"], V.tensor_copy, T.offa[:], T.asum[:])
    op("v", ["jrow", "pc4"], ["cb"], V.tensor_scalar, T.cb[:], T.jrow[:, 0:8], 1024.0, pc(4), A.mult, A.add)
    op("v", ["ct"], ["qc"], V.quantize_mx, T.qc[:], T.sc[:], T.ct[:])

    def x_parts(h):
        for b in range(4):
            o = 512 * b + 256 * h
            op("s", ["xs", "offx%d" % b], ["xh%d_%d" % (b, h)], S.activation, T.xh[:, o:o + 256],
               T.xs[:, 0:1024].indirect(T.offx[:, 32 * b + 16 * h:32 * b + 16 * h + 16]), ACT.Copy, scale=0.5)

    def output_constants():
        op("v", ["jrow", "pc3"], ["offn"], V.tensor_scalar, T.offn[:], T.jrow[:, 0:16:2], pc(3), None, A.add)
        op("v", ["pc3"], ["pc7"], V.tensor_scalar, pc(7), pc(3), 4.0, None, A.mult)
        op("v", ["vs"], ["qv"], V.quantize_mx, T.qv[:], T.sv[:], T.vs[:])
        op("v", ["pat2", "pc7"], ["offm"], V.tensor_scalar, T.offm[:], T.pat[:, 32:64], pc(7), None, A.add)
        op("v", [], ["base"], V.memset, T.base[:, 0:64], float(64 * ((rank - ROUNDS) % n_ranks)))
        op("v", [], ["base2"], V.memset, T.base[:, 64:128], float(64 * ((rank + ROUNDS) % n_ranks)))

    def picked_origins():
        op("s", ["oin", "offf"], ["org"], S.activation, T.org[:], T.oin[:, 0:512].indirect(T.offf[:, 0:8]), ACT.Copy)

    four = [(f, h) for f in range(2) for h in range(2)]
    for t in range(ROUNDS):
        last = t == ROUNDS - 1
        qzy, szy, qin, sin, lst, lin = [T[k + str(t)] for k in ("qzy", "szy", "qin", "sin", "lst", "lin")]

        def scorers():
            for b in range(4):
                op("s", ["bh%d" % b, "offs0", "offs1"], ["st%d" % b], S.activation, T.st[:, b:1024:4],
                   T.bh[:, 144 * b:144 * b + 144].indirect(T.offs[:, 0:16]), ACT.Copy, scale=2.0)

        def candidates(h):
            for b in range(4):
                o = 512 * b + 256 * h
                op("v", ["bh%d" % b, "xh%d_%d" % (b, h), "offa"], ["zy%d_%d" % (b, h)], V.tensor_tensor,
                   T.zy[:, 1024 * h + b:1024 * h + 1024:4],
                   T.bh[:, 144 * b:144 * b + 128].indirect(T.offa[:, 16 * h:16 * h + 16]), T.xh[:, o:o + 256], A.add)

        def scores(h):
            if h == 0:
                op("v", ["st%d" % b for b in range(4)], ["qs"], V.quantize_mx, T.qs[:], T.ss[:], T.st[:])
            for f in range(2):
                c, o = 256 * f + 128 * h, 1024 * h + 512 * f
                op("v", ["zy%d_%d" % (b, h) for b in range(4)], ["qzy%d_%d" % (f, h)], V.quantize_mx, qzy[:, c:c + 128],
                   szy[:, c:c + 128], T.zy[:, o:o + 512])
            for f in range(2):
                c = 256 * f + 128 * h
                op("p", ["qs", "qzy%d_%d" % (f, h)], ["pss%d" % h], P.matmul_mx, T.pss[:, 512 * h:512 * h + 128],
                   T.qs[:, 128 * f:128 * f + 128], T.ss[:, 128 * f:128 * f + 128], qzy[:, c:c + 128], szy[:, c:c + 128],
                   f == 0, f == 1)

        def rows(h):
            op("s", [], ["pss%d" % h, "rows%d" % h], S.activation, T.rows[:, 128 * h:128 * h + 128],
               T.pss[:, 512 * h:512 * h + 128], ACT.Copy)
            op("s", ["rows%d" % h, "offp"], ["piv%d" % h], S.activation, T.piv[:, 16 * h:16 * h + 16],
               T.rows[:, 128 * h:128 * h + 128].indirect(T.offp[:, 0:1]), ACT.Copy)

        def origins():
            if t > 0:
                picked_origins()
            op("s", ["org", "offa"], ["ozy"], S.activation, T.ozy[:], T.org[:, 0:128].indirect(T.offa[:, 0:32]),
               ACT.Copy)
            dmas("y", "oa%d" % t, ["ozy"], ["oout"],
                 [(T.oout[2 * t + f, 64 * h:64 * h + 64, :], T.ozy[0:128:16, 256 * h + 128 * f:256 * h + 128 * f + 128])
                  for f, h in four])

        def move_origins():
            send("ao%d" % t, ["oout"], "oland", (T.oout[2 * t], T.oland[2 * t]),
                 (T.oout[2 * t + 1], T.oland[2 * t + 1]))
            dmas("y", "ob%d" % t, ["oland"], ["oin"],
                 [(T.oin[0:128:16, 256 * f + 128 * h:256 * f + 128 * h + 128], T.oland[2 * t + f, 64 * h:64 * h + 64, :])
                  for f, h in four])

        def lane(q, lo, hi, b):
            return ["sig%d_%d_%d" % (q, k, b) for k in range(lo, hi)]

        def blocks(q, lo, hi):
            return [k for b in range(4) for k in lane(q, lo, hi, b)]

        def seen(q, lo, hi):
            return ["piv%d" % (q // 4)] + ["rows%d" % h for h in range(lo // 4, (hi - 1) // 4 + 1)]

        def signs(q, lo, hi):
            for b in range(4):
                op("s", seen(q, lo, hi), lane(q, lo, hi, b), S.activation,
                   T.sig[:, 1024 * q + 128 * lo + b:1024 * q + 128 * hi:4], T.rows[:, 32 * lo:32 * hi], ACT.Sign,
                   bias=T.piv[:, 4 * q + b:4 * q + b + 1], scale=-1.0)

        def direct(q, lo, hi):
            for b in range(4):
                op("v", seen(q, lo, hi), lane(q, lo, hi, b), V.tensor_scalar,
                   T.sig[:, 1024 * q + 128 * lo + b:1024 * q + 128 * hi:4], T.rows[:, 32 * lo:32 * hi],
                   T.piv[:, 4 * q + b:4 * q + b + 1], None, A.is_le if lo > q else A.is_lt)

        def decide(q, lo, hi):
            if lo <= q < hi:
                v = T.sig[:, 1152 * q:1152 * q + 128]
                op("v", ["tau"], blocks(q, q, q + 1), V.tensor_tensor, v, v, T.tau[:], A.is_gt)
            for a, b, how in ((lo, min(hi, q), A.is_gt), (max(lo, q + 1), hi, A.is_ge)):
                if a < b:
                    v = T.sig[:, 1024 * q + 128 * a:1024 * q + 128 * b]
                    op("v", [], blocks(q, a, b), V.tensor_scalar, v, v, 0.0, None, how)

        def relu(q, lo, hi):
            v = T.sig[:, 1024 * q + 128 * lo:1024 * q + 128 * hi]
            op("s", [], blocks(q, lo, hi), S.activation, v, v, ACT.Relu)

        done = []

        def count(q):
            op("v", blocks(q, 0, 8), ["qg%d" % q], V.quantize_mx, T.qg[:, 256 * q:256 * q + 256],
               T.sg[:, 256 * q:256 * q + 256], T.sig[:, 1024 * q:1024 * q + 1024])
            op("p", ["qc", "qg%d" % q], ["psr"], P.matmul_mx, T.psr[:, 0:256], T.qc[:], T.sc[:],
               T.qg[:, 256 * q:256 * q + 256], T.sg[:, 256 * q:256 * q + 256], len(done) == 0, len(done) == 7)
            done.append(q)
            if t == 0 and len(done) == CFG["unpack"] - 1:
                op("v", ["et%d" % b for b in range(4)], ["qe"], V.quantize_mx, T.qe[:], T.se[:], T.et[:])
            if len(done) == CFG["unpack"]:
                for b in range(4):
                    op("p", ["qe", "qin"], ["psd%d" % b], P.matmul_mx, T.psd[:, 512 * b:512 * b + 512],
                       T.qe[:, 128 * b:128 * b + 128], T.se[:, 128 * b:128 * b + 128], qin[:], sin[:], True, True)

        scorers()
        if t == 0:
            x_parts(0)
            x_parts(1)
        if last:
            origins()
        candidates(0)
        scores(0)
        candidates(1)
        rows(0)
        for q in range(CFG["early"]):
            signs(q, 0, 4)
        scores(1)
        send("ac%d" % t, ["qzy%d_%d" % fh for fh in four], "qin", (u8(qzy[:, 0:256]), u8(qin[:, 0:256])),
             (u8(qzy[:, 256:512]), u8(qin[:, 256:512])))
        send("ac%d" % t, [], "qin", (szy[:, 0:256], sin[:, 0:256]), (szy[:, 256:512], sin[:, 256:512]))
        if last:
            move_origins()
        rows(1)
        for step, q, lo, hi in PLAN:
            if step == "count":
                count(q)
            elif step == "origins":
                if 0 < t < ROUNDS - 1:
                    origins()
                    move_origins()
            else:
                {"signs": signs, "direct": direct, "decide": decide, "relu": relu}[step](q, lo, hi)
        op("v", [], ["psr", "rk"], V.tensor_copy, T.rk[:], T.psr[:, 0:256])
        for n in range(8):
            v = T.dif[:, 256 * n:256 * n + 256]
            if n < 8 - CFG["ns"]:
                op("v", ["rk", "cb"], ["dif%d" % n], V.tensor_scalar, v, T.rk[:], T.cb[:, n:n + 1], 1024.0,
                   A.not_equal, A.mult)
            else:
                op("s", ["rk", "cb"], ["dif%d" % n], S.activation, v, T.rk[:], ACT.Abs, bias=T.cb[:, n:n + 1],
                   scale=-1.0)
        cuts = CFG["cuts"]
        for lo, hi in zip(cuts, cuts[1:]):
            op("v", ["ones"] + ["dif%d" % n for n in range(lo, hi)], ["run%d" % lo], V.tensor_tensor_scan,
               T.run[:, 256 * lo:256 * hi], T.dif[:, 256 * lo:256 * hi], T.ones[:, 0:256 * (hi - lo)], 0.0,
               A.min, A.add)
        runs = ["run%d" % n for n in cuts[:-1]]
        ends = T.run[:, 255:2048:256]
        op("v", runs + ["pc12", "pc13"], ["lsta"], V.tensor_scalar, lst[:, 0:8], ends, pc(12), pc(13), A.mult, A.add)
        op("v", runs + ["pc14", "pc6"], ["lstb"], V.tensor_scalar, lst[:, 8:16], ends, pc(14), pc(6), A.mult, A.add)
        send("al%d" % t, ["lsta", "lstb"], "lin", (lst[:, 0:8], lin[:, 0:8]), (lst[:, 8:16], lin[:, 8:16]))
        for b in range(4):
            out, src = T.dp[:, 512 * b:512 * b + 512], T.psd[:, 512 * b:512 * b + 512]
            if b < 2:
                op("v", [], ["psd%d" % b, "dp%d" % b], V.tensor_copy, out, src)
            else:
                op("s", [], ["psd%d" % b, "dp%d" % b], S.activation, out, src, ACT.Copy)
        if t == 0:
            origins()
            move_origins()
            output_constants()
        op("v", ["lin"], ["lsum"], V.tensor_tensor, T.lsum[:], lin[:, 0:8], lin[:, 8:16], A.add)
        op("v", ["lsum", "pc6"], ["offf"], V.tensor_scalar, T.offf[:], T.lsum[:], pc(6), None, A.add)
        for b in range(4):
            out, src = T.ft[:, b:512:4], T.dp[:, 512 * b:512 * b + 512].indirect(T.offf[:, 0:8])
            if b < 2:
                op("v", ["dp%d" % b, "offf"], ["ft%d" % b], V.tensor_copy, out, src)
            else:
                op("s", ["dp%d" % b, "offf"], ["ft%d" % b], S.activation, out, src, ACT.Copy)
        fts = ["ft%d" % b for b in range(4)]
        op("v", fts, ["qf"], V.quantize_mx, T.qf[:], T.sf[:], T.ft[:])
        if last:
            op("s", fts + ["offm", "fh"], ["fh3"], S.activation, T.fh[:, 384:512],
               T.ft[:, 0:512].indirect(T.offm[:, 24:32]), ACT.Copy)
            op("v", fts + ["offm"], ["fh"], V.tensor_copy, T.fh[:, 0:384], T.ft[:, 0:512].indirect(T.offm[:, 0:24]))
        else:
            op("v", fts, ["fh"], V.tensor_scalar, T.fh[:], T.ft[:], 0.5, None, A.mult)
        for b in range(4):
            op("p", ["qw", "qf"], ["psd%d" % b], P.matmul_mx, T.psd[:, 512 * b:512 * b + 128],
               T.qw[:, 128 * b:128 * b + 128], T.sw[:, 128 * b:128 * b + 128], T.qf[:], T.sf[:], True, True)
        for b in range(4):
            rl = T.rl[:, 128 * b:128 * b + 128]
            op("s", [], ["psd%d" % b, "rl%d" % b], S.activation, rl, T.psd[:, 512 * b:512 * b + 128], ACT.Relu,
               scale=0.03125 if last else 0.015625)
            if last:
                op("v", ["rl%d" % b, "fh", "fh3", "offn"], ["bt%d" % b], V.tensor_tensor, T.bt[:, b:512:4],
                   rl.indirect(T.offn[:, 0:8]), T.fh[:, 128 * b:128 * b + 128], A.add)
            else:
                op("v", ["rl%d" % b, "fh"], ["bh%d" % b], V.tensor_tensor, T.bh[:, 144 * b:144 * b + 128], rl,
                   T.fh[:, b:512:4], A.add)

    picked_origins()
    op("v", ["bt%d" % b for b in range(4)], ["qb"], V.quantize_mx, T.qb[:], T.sb[:], T.bt[:])
    op("p", ["qv", "qb"], ["pss0"], P.matmul_mx, T.pss[:, 0:128], T.qv[:], T.sv[:], T.qb[:], T.sb[:], True, True)
    op("v", ["org", "offn", "base", "base2"], ["otb"], V.tensor_tensor, T.otb[:],
       T.org[:, 0:128].indirect(T.offn[:, 0:8]), T.base[:], A.add)
    dmas("y", "stc", ["qb"], [], [(T.oc[:], u8(T.qb[:]))] +
         [(T.osc[4 * k:4 * k + 4, :], T.sb[32 * k:32 * k + 4, :]) for k in range(4)])
    op("s", [], ["pss0", "yb"], S.activation, T.yb[:], T.pss[:, 0:128], ACT.Copy)
    dmas("s", "sty", ["yb"], [], [(T.y[:], T.yb[:])])
    dmas("y", "sto", ["otb"], [], [(T.ot[:], T.otb[0:128:16, :])])
    for sem, val in total.items():
        g.wait_ge(T.sem[sem], val)
